import numpy as np, ml_dtypes
CORES = [4,20,60,84,92,100,116]
N = 7
import mx_ref
NC, G = 256, 4
BF = ml_dtypes.bfloat16
def cut(t, i, w=512):
    return t[:, w * i:w * i + w]
def tile(rs):
    return np.stack(rs, axis=2).reshape(128, -1).astype(BF)
def layer(w, X):
    out = []
    for i in range(G):
        for t in range(len(X)):
            p = mx_ref.matmul(mx_ref.quantize(cut(w, len(X) * i + t)), X[t])
            z = p if t == 0 else z + p
        out.append(z)
    return out
def scaled(Z, s):
    return [z * s for z in Z]
def setup_inputs(rng):
    def f(*shape):
        return mx_ref.flush((rng.standard_normal(shape, dtype=np.float32) * np.exp2(rng.integers(-2, 3, shape[:-1] + (1,)))).astype(BF))
    return {"x": f(N, 128, 4 * NC), "w1": f(N, 128, G * 512), "w2": f(N, 128, 512)}
def setup_inputs_blocks(rng):
    d = setup_inputs(rng)
    for k in ("w2",): d[k] = mx_ref.spread(d[k], rng, 4)
    for k in ("x", "w1"): d[k] = mx_ref.spread(d[k], rng, 2)
    return d
def setup_inputs_wide(rng):
    d = setup_inputs(rng)
    for k in ("x", "w1", "w2"): d[k] = mx_ref.flush((d[k].astype(np.float32) * np.exp2(rng.integers(-3, 4, (N, 1, 1))).astype(np.float32)).astype(BF))
    return d
def reference(x, w1, w2, own=None):
    Z = [layer(w1[r], [mx_ref.quantize(x[r])]) for r in range(N)]
    a = max(float(np.abs(z).max()) for r in range(N) for z in Z[r])
    s = np.float32(1 / a)
    h = np.stack([tile(scaled(Z[r], s)) for r in range(N)])
    use = h if own is None else own["h"]
    H = [mx_ref.quantize(use[j]) for j in range(N)]
    y = np.zeros((N, 128, N * NC), np.float32)
    for r in range(N):
        qw = mx_ref.quantize(w2[r])
        for j in range(N):
            y[r][:, NC * j:NC * j + NC] = mx_ref.matmul(qw, H[j])
    return {"h": h, "y": y}

@@ -1,0 +1,255 @@
+from concourse.bass import DstId, RemoteDMATransfer
+from concourse.mybir import dt, AluOpType, AxisListType, ActivationFunctionType
+
+N = 7
+NC = 256
+OWN = 4
+
+SCRATCH = {
+    "xt": ("sbuf", [128, 4 * NC], "bfloat16"),
+    "w1t": ("sbuf", [128, 2048], "bfloat16"),
+    "w2t": ("sbuf", [128, 512], "bfloat16"),
+    "xq": ("sbuf", [128, NC], "float8_e4m3fn_x4"),
+    "xs": ("sbuf", [128, NC], "uint8"),
+    "w1q": ("sbuf", [128, 512], "float8_e4m3fn_x4"),
+    "w1s": ("sbuf", [128, 512], "uint8"),
+    "w2q": ("sbuf", [128, 128], "float8_e4m3fn_x4"),
+    "w2s": ("sbuf", [128, 128], "uint8"),
+    "ones": ("sbuf", [128, 128], "float32"),
+    "eye": ("sbuf", [128, 128], "float32"),
+    "zero": ("sbuf", [128, 128], "float32"),
+    "bc": ("sbuf", [128, 128], "float32"),
+    "pm": ("sbuf", [128, 4], "float32"),
+    "m3": ("sbuf", [128, 1], "float32"),
+    "land": ("sbuf", [128, OWN + N - 1], "float32"),
+    "amax": ("sbuf", [128, 1], "float32"),
+    "inv": ("sbuf", [128, 1], "float32"),
+    "ht": ("sbuf", [128, 4 * NC], "bfloat16"),
+    "hq": ("sbuf", [128, N * NC], "float8_e4m3fn_x4"),
+    "hs": ("sbuf", [128, N * NC], "uint8"),
+    "yt": ("sbuf", [128, N * NC], "float32"),
+    "rm": ("sbuf", [128, 1], "float32"),
+    "rq": ("sbuf", [128, NC], "float8_e4m3fn_x4"),
+    "rs": ("sbuf", [128, NC], "uint8"),
+    "ps": ("psum", [128, 512 * 8], "float32"),
+}
+SEMAPHORES = (["lx", "la", "lb", "lw", "f1", "f2", "f3", "eyed", "qx", "qw", "qh", "bcd", "tr", "own", "mx", "am", "inv",
+               "m3d", "stored", "left", "left1", "rmx", "rcode", "rscale"]
+              + ["q%d" % i for i in range(4)] + ["z%d" % i for i in range(4)] + ["r%d" % i for i in range(4)]
+              + ["sc%d" % i for i in range(4)] + ["arr%d" % i for i in range(N)]
+              + ["p%d" % i for i in range(N + 1)] + ["c%d" % i for i in range(N + 1)])
+
+
+def helpers(core, topo):
+    every = range(topo.CHIPS * topo.CORES_PER_CHIP)
+    own = [c for c in every if c != core and topo.chip(c) == topo.chip(core)
+           and all(topo.may_write(c, d) for d in every if d != c)]
+    return ([c for c in own if topo.die(c) == topo.die(core)],
+            [c for c in own if topo.die(c) != topo.die(core)])
+
+
+def plan(T, topo):
+    ways = []
+    for s in range(N):
+        near, far = helpers(T.cores[s], topo)
+        ring = [(s + k) % N for k in range(1, N)]
+        peers = [d for d in ring if topo.same_plane(topo.chip(T.cores[s]), topo.chip(T.cores[d]))]
+        mine = sorted(peers + [s])
+        across = [d for d in range(N) if d not in mine]
+        i = mine.index(s)
+        if len(across) <= 2:
+            k = i % len(across)
+            across = across[k:] + across[:k]
+            w = {peers[0]: None, peers[1]: None, across[0]: near[0], peers[2]: near[0],
+                 peers[3]: far[0], across[1]: far[0]}
+        else:
+            k = (2 * i) % len(across)
+            across = across[k:] + across[:k]
+            w = {d: None for d in peers}
+            for d, h in zip(across, (near[0], near[0], far[0], far[0], near[1])):
+                w[d] = h
+        ways.append(w)
+    return ways
+
+
+def count(mask):
+    return bin(mask).count("1")
+
+
+def send(g, topo, T, core, src, dsts, mask, sem, left):
+    ids = []
+    for c, _ in dsts:
+        rid, pid, _e = topo.addr(c)
+        ids.append(DstId(rid=rid, pnc=pid))
+    g.remote_dma_fused([RemoteDMATransfer(dst_ids=ids, dma_engine_mask=mask, remote_sem=sem, srcs=[src],
+                                          dsts=[ap for _, ap in dsts], alu_op=0)], local_sem=left)
+
+
+def slot(s, r):
+    k = OWN + (s if s < r else s - 1)
+    return slice(k, k + 1)
+
+
+def block(s):
+    return slice(NC * s, NC * (s + 1))
+
+
+def rank_program(g, core, T, topo):
+    ways = plan(T, topo)
+    rank = T.rank_of(core)
+    if rank is None:
+        for s in range(N):
+            to = [d for d in ways[s] if ways[s][d] == core]
+            if to:
+                relay(g, core, T, topo, s, to)
+        return
+    S = T.sem
+    MULT, MAX = AluOpType.mult, AluOpType.max
+    X, COPY = AxisListType.X, ActivationFunctionType.Copy
+    v, pe, act, sp = g.vector, g.tensor, g.scalar, g.sync
+    w = ways[rank]
+    direct = [d for d in w if w[d] is None]
+    relays = []
+    for d in w:
+        if w[d] is not None and w[d] not in relays:
+            relays.append(w[d])
+    inside = topo.mask(core, relays[0])
+    outside = topo.mask(core, T.cores[direct[0]])
+    upper = inside & ~outside
+
+    sp.dma_start(T.xt[:], T.x[:]).then_inc(S.lx, 16)
+    act.dma_start(T.w1t[:, 0:1024], T.w1[:, 0:1024]).then_inc(S.la, 16)
+    sp.dma_start(T.w1t[:, 1024:2048], T.w1[:, 1024:2048]).then_inc(S.lb, 16)
+    sp.dma_start(T.w2t[:], T.w2[:]).then_inc(S.lw, 16)
+
+    v.memset(T.ones[:], 1.0).then_inc(S.f1, 1)
+    v.memset(T.zero[:], 0.0).then_inc(S.f2, 1)
+    v.memset(T.land[:, 0:OWN], 0.0).then_inc(S.f3, 1)
+    g.wait_ge(S.f1, 1)
+    g.affine_select(T.eye[:], T.ones[:], [[-1, 128]], AluOpType.is_equal, 0.0, 0, 1).then_inc(S.eyed, 1)
+
+    def quant_w1(i):
+        v.quantize_mx(T.w1q[:, 128 * i:128 * i + 128], T.w1s[:, 128 * i:128 * i + 128],
+                      T.w1t[:, 512 * i:512 * i + 512]).then_inc(S["q%d" % i], 1)
+
+    def size(i):
+        v.wait_ge(S["z%d" % i], 1)
+        v.tensor_reduce(T.pm[:, i:i + 1], T.ps[:, 512 * i:512 * i + NC], X, MAX,
+                        apply_absolute_value=True).then_inc(S["r%d" % i], 1)
+
+    pe.wait_ge(S.qx, 1)
+    for i in range(4):
+        pe.wait_ge(S["q%d" % i], 1)
+        pe.matmul_mx(T.ps[:, 512 * i:512 * i + NC], T.w1q[:, 128 * i:128 * i + 128], T.w1s[:, 128 * i:128 * i + 128],
+                     T.xq[:], T.xs[:], True, True).then_inc(S["z%d" % i], 1)
+    v.wait_ge(S.lx, 16)
+    v.quantize_mx(T.xq[:], T.xs[:], T.xt[:]).then_inc(S.qx, 1)
+    v.wait_ge(S.la, 16)
+    quant_w1(0)
+    quant_w1(1)
+    size(0)
+    v.wait_ge(S.lb, 16)
+    quant_w1(2)
+    quant_w1(3)
+    size(1)
+    size(2)
+    for i in range(3):
+        v.wait_ge(S["r%d" % i], 1)
+    v.tensor_reduce(T.m3[:], T.pm[:, 0:3], X, MAX).then_inc(S.m3d, 1)
+    size(3)
+    v.wait_ge(S.f2, 1)
+    v.wait_ge(S.m3d, 1)
+    v.wait_ge(S.r3, 1)
+    v.tensor_scalar(T.bc[:], T.zero[:], T.pm[:, 3:4], T.m3[:], MAX, MAX).then_inc(S.bcd, 1)
+    pe.wait_ge(S.eyed, 1)
+    pe.wait_ge(S.bcd, 1)
+    pe.matmul(T.ps[:, 2048:2048 + 128], T.bc[:], T.eye[:], True, True).then_inc(S.tr, 1)
+    v.wait_ge(S.f3, 1)
+    v.wait_ge(S.tr, 1)
+    v.tensor_reduce(T.land[:, 0:1], T.ps[:, 2048:2048 + 128], X, MAX).then_inc(S.own, 1)
+
+    g.wait_ge(S.own, 1)
+    send(g, topo, T, core, T.land[:, 0:1], [(h, T.rm[:]) for h in relays], upper, S.rmx, S.left1)
+    send(g, topo, T, core, T.land[:, 0:1], [(T.cores[d], T.land[:, slot(rank, d)]) for d in direct],
+         outside, S.mx, S.left1)
+    v.wait_ge(S.lw, 16)
+    v.quantize_mx(T.w2q[:], T.w2s[:], T.w2t[:]).then_inc(S.qw, 1)
+    v.wait_ge(S.own, 1)
+    arrive = 0
+    for s in range(N):
+        if s != rank:
+            via = ways[s][rank]
+            arrive += count(topo.mask(T.cores[s] if via is None else via, core))
+    v.wait_ge(S.mx, arrive)
+    v.tensor_reduce(T.amax[:], T.land[:], X, MAX).then_inc(S.am, 1)
+    v.wait_ge(S.am, 1)
+    v.reciprocal(T.inv[:], T.amax[:]).then_inc(S.inv, 1)
+
+    v.wait_ge(S.inv, 1)
+    act.wait_ge(S.inv, 1)
+    for b in (0, 1):
+        v.tensor_scalar(T.ht[:, b:4 * NC:4], T.ps[:, 512 * b:512 * b + NC], T.inv[:], None,
+                        MULT).then_inc(S["sc%d" % b], 1)
+    for b in (2, 3):
+        act.activation(T.ht[:, b:4 * NC:4], T.ps[:, 512 * b:512 * b + NC], COPY,
+                       scale=T.inv[:]).then_inc(S["sc%d" % b], 1)
+    for b in range(4):
+        v.wait_ge(S["sc%d" % b], 1)
+    v.quantize_mx(T.hq[:, block(rank)], T.hs[:, block(rank)], T.ht[:]).then_inc(S.qh, 1)
+
+    codes, scales = T.hq[:, block(rank)].bitcast(dt.uint8), T.hs[:, block(rank)]
+    g.wait_ge(S.qh, 1)
+    send(g, topo, T, core, codes, [(h, T.rq[:].bitcast(dt.uint8)) for h in relays], inside, S.rcode, S.left)
+    send(g, topo, T, core, scales, [(h, T.rs[:]) for h in relays], inside, S.rscale, S.left)
+    sem = S["arr%d" % rank]
+    send(g, topo, T, core, codes, [(T.cores[d], codes) for d in direct], outside, sem, S.left)
+    send(g, topo, T, core, scales, [(T.cores[d], scales) for d in direct], outside, sem, S.left)
+    g.wait_ge(S.left1, count(upper) + count(outside))
+
+    order = ([rank] + [s for s in range(N) if s != rank and ways[s][rank] is None]
+             + [s for s in range(N) if s != rank and ways[s][rank] is not None])
+    banks = [5, 6, 7, 0, 1, 2, 3, 4]
+    sp.wait_ge(S.left, 2 * count(inside) + 2 * count(outside))
+    for b in range(4):
+        sp.wait_ge(S["sc%d" % b], 1)
+    sp.dma_start(T.h[:], T.ht[:]).then_inc(S.stored, 16)
+    pe.wait_ge(S.qw, 1)
+    for k, s in enumerate(order):
+        if s == rank:
+            pe.wait_ge(S.qh, 1)
+        else:
+            via = ways[s][rank]
+            pe.wait_ge(S["arr%d" % s], 2 * count(topo.mask(T.cores[s] if via is None else via, core)))
+        last = k == N - 1
+        parts = ([(NC * s, NC // 2, k), (NC * s + NC // 2, NC // 2, k + 1)] if last else [(NC * s, NC, k)])
+        for c0, n, m in parts:
+            out = T.ps[:, 512 * banks[m]:512 * banks[m] + n]
+            pe.matmul_mx(out, T.w2q[:], T.w2s[:], T.hq[:, c0:c0 + n], T.hs[:, c0:c0 + n],
+                         True, True).then_inc(S["p%d" % m], 1)
+            if m % 2 == 0:
+                v.wait_ge(S["p%d" % m], 1)
+                v.tensor_copy(T.yt[:, c0:c0 + n], out).then_inc(S["c%d" % m], 1)
+            else:
+                act.wait_ge(S["p%d" % m], 1)
+                act.activation(T.yt[:, c0:c0 + n], out, COPY).then_inc(S["c%d" % m], 1)
+            sp.wait_ge(S["c%d" % m], 1)
+        sp.dma_start(T.y[:, block(s)], T.yt[:, block(s)]).then_inc(S.stored, 16)
+    sp.wait_ge(S.stored, 16 * (N + 1))
+
+
+def relay(g, core, T, topo, s, to):
+    S = T.sem
+    src = T.cores[s]
+    first = [d for d in range(N) if d != s and topo.same_plane(topo.chip(src), topo.chip(T.cores[d]))][0]
+    inside = topo.mask(src, core)
+    upper = inside & ~topo.mask(src, T.cores[first])
+    mask = topo.mask(core, T.cores[to[0]])
+    g.wait_ge(S.rmx, count(upper))
+    send(g, topo, T, core, T.rm[:], [(T.cores[d], T.land[:, slot(s, d)]) for d in to], mask, S.mx, S.left)
+    sem = S["arr%d" % s]
+    g.wait_ge(S.rcode, count(inside))
+    send(g, topo, T, core, T.rq[:].bitcast(dt.uint8),
+         [(T.cores[d], T.hq[:, block(s)].bitcast(dt.uint8)) for d in to], mask, sem, S.left)
+    g.wait_ge(S.rscale, count(inside))
+    send(g, topo, T, core, T.rs[:], [(T.cores[d], T.hs[:, block(s)]) for d in to], mask, sem, S.left)
+    g.wait_ge(S.left, 3 * count(mask))

@@ -4,6 +4,14 @@ from concourse.mybir import dt, AluOpType, AxisListType, ActivationFunctionType
 N = 7
 NC = 256
 OWN = 4
+WAYS = ("2n 4n 3f 5D 1D 6f",
+        "3D 2f 6g 0f 5D 4g",
+        "6f 0M 5f 4D 1n 3n",
+        "1g 5D 6D 2g 0n 4n",
+        "6n 0f 1f 5m 3n 2D",
+        "6D 4n 1f 3f 2n 0D",
+        "3g 2g 0D 1D 4f 5f")
+TURN = ("654132", "350264", "104356", "160425", "652310", "031264", "524130")
 
 SCRATCH = {
     "xt": ("sbuf", [128, 4 * NC], "bfloat16"),
@@ -16,11 +24,11 @@ SCRATCH = {
     "w2q": ("sbuf", [128, 128], "float8_e4m3fn_x4"),
     "w2s": ("sbuf", [128, 128], "uint8"),
     "ones": ("sbuf", [128, 128], "float32"),
-    "eye": ("sbuf", [128, 128], "float32"),
-    "zero": ("sbuf", [128, 128], "float32"),
-    "bc": ("sbuf", [128, 128], "float32"),
-    "pm": ("sbuf", [128, 4], "float32"),
-    "m3": ("sbuf", [128, 1], "float32"),
+    "sel": ("sbuf", [128, 16], "float32"),
+    "pm": ("sbuf", [128, 32], "float32"),
+    "pmt": ("sbuf", [128, 32], "float32"),
+    "gm": ("sbuf", [128, 1], "float32"),
+    "spread": ("sbuf", [128, 16], "float32"),
     "land": ("sbuf", [128, OWN + N - 1], "float32"),
     "amax": ("sbuf", [128, 1], "float32"),
     "inv": ("sbuf", [128, 1], "float32"),
@@ -33,41 +41,35 @@ SCRATCH = {
     "rs": ("sbuf", [128, NC], "uint8"),
     "ps": ("psum", [128, 512 * 8], "float32"),
 }
-SEMAPHORES = (["lx", "la", "lb", "lw", "f1", "f2", "f3", "eyed", "qx", "qw", "qh", "bcd", "tr", "own", "mx", "am", "inv",
-               "m3d", "stored", "left", "left1", "rmx", "rcode", "rscale"]
+SEMAPHORES = (["lx", "la", "lb", "lw", "f1", "f2", "f3", "seld", "qx", "qw", "qh", "pmtd", "gmd", "spd", "tr", "own",
+               "mx", "am", "inv", "stored", "left", "left1", "rcode", "rscale"]
               + ["q%d" % i for i in range(4)] + ["z%d" % i for i in range(4)] + ["r%d" % i for i in range(4)]
               + ["sc%d" % i for i in range(4)] + ["arr%d" % i for i in range(N)]
               + ["p%d" % i for i in range(N + 1)] + ["c%d" % i for i in range(N + 1)])
 
 
-def helpers(core, topo):
+def mate_port_cores(chip, topo):
     every = range(topo.CHIPS * topo.CORES_PER_CHIP)
-    own = [c for c in every if c != core and topo.chip(c) == topo.chip(core)
-           and all(topo.may_write(c, d) for d in every if d != c)]
-    return ([c for c in own if topo.die(c) == topo.die(core)],
-            [c for c in own if topo.die(c) != topo.die(core)])
+    return [c for c in every if topo.chip(c) == chip and all(topo.may_write(c, d) for d in every if d != c)]
 
 
 def plan(T, topo):
     ways = []
     for s in range(N):
-        near, far = helpers(T.cores[s], topo)
-        ring = [(s + k) % N for k in range(1, N)]
-        peers = [d for d in ring if topo.same_plane(topo.chip(T.cores[s]), topo.chip(T.cores[d]))]
-        mine = sorted(peers + [s])
-        across = [d for d in range(N) if d not in mine]
-        i = mine.index(s)
-        if len(across) <= 2:
-            k = i % len(across)
-            across = across[k:] + across[:k]
-            w = {peers[0]: None, peers[1]: None, across[0]: near[0], peers[2]: near[0],
-                 peers[3]: far[0], across[1]: far[0]}
-        else:
-            k = (2 * i) % len(across)
-            across = across[k:] + across[:k]
-            w = {d: None for d in peers}
-            for d, h in zip(across, (near[0], near[0], far[0], far[0], near[1])):
-                w[d] = h
+        me = T.cores[s]
+        own = mate_port_cores(topo.chip(me), topo)
+        near = [c for c in own if c != me and topo.die(c) == topo.die(me)]
+        far = [c for c in own if topo.die(c) != topo.die(me)]
+        w = {}
+        for way in WAYS[s].split():
+            d, how = int(way[0]), way[1]
+            if how == "D":
+                w[d] = None
+            elif how in "mM":
+                mate = [c for c in range(topo.CHIPS) if topo.mates(c, topo.chip(T.cores[d]))][0]
+                w[d] = [c for c in mate_port_cores(mate, topo) if (topo.die(c) == topo.die(me)) == (how == "m")][0]
+            else:
+                w[d] = {"n": near[0], "f": far[0], "g": far[1]}[how]
         ways.append(w)
     return ways
 
@@ -76,7 +78,7 @@ def count(mask):
     return bin(mask).count("1")
 
 
-def send(g, topo, T, core, src, dsts, mask, sem, left):
+def send(g, topo, src, dsts, mask, sem, left):
     ids = []
     for c, _ in dsts:
         rid, pid, _e = topo.addr(c)
@@ -94,6 +96,13 @@ def block(s):
     return slice(NC * s, NC * (s + 1))
 
 
+def masks(T, topo, w, rank):
+    me = T.cores[rank]
+    inside = [topo.mask(me, h) for h in w.values() if h is not None and topo.chip(h) == topo.chip(me)][0]
+    outside = [topo.mask(me, T.cores[d]) for d in w if w[d] is None][0]
+    return inside, outside, inside & ~outside
+
+
 def rank_program(g, core, T, topo):
     ways = plan(T, topo)
     rank = T.rank_of(core)
@@ -101,7 +110,7 @@ def rank_program(g, core, T, topo):
         for s in range(N):
             to = [d for d in ways[s] if ways[s][d] == core]
             if to:
-                relay(g, core, T, topo, s, to)
+                relay(g, core, T, topo, ways, s, to)
         return
     S = T.sem
     MULT, MAX = AluOpType.mult, AluOpType.max
@@ -109,13 +118,11 @@ def rank_program(g, core, T, topo):
     v, pe, act, sp = g.vector, g.tensor, g.scalar, g.sync
     w = ways[rank]
     direct = [d for d in w if w[d] is None]
-    relays = []
-    for d in w:
-        if w[d] is not None and w[d] not in relays:
-            relays.append(w[d])
-    inside = topo.mask(core, relays[0])
-    outside = topo.mask(core, T.cores[direct[0]])
-    upper = inside & ~outside
+    relays, remote = [], []
+    for h in w.values():
+        if h is not None and h not in relays + remote:
+            (relays if topo.chip(h) == topo.chip(core) else remote).append(h)
+    inside, outside, upper = masks(T, topo, w, rank)
 
     sp.dma_start(T.xt[:], T.x[:]).then_inc(S.lx, 16)
     act.dma_start(T.w1t[:, 0:1024], T.w1[:, 0:1024]).then_inc(S.la, 16)
@@ -123,10 +130,10 @@ def rank_program(g, core, T, topo):
     sp.dma_start(T.w2t[:], T.w2[:]).then_inc(S.lw, 16)
 
     v.memset(T.ones[:], 1.0).then_inc(S.f1, 1)
-    v.memset(T.zero[:], 0.0).then_inc(S.f2, 1)
+    v.memset(T.pm[:], 0.0).then_inc(S.f2, 1)
     v.memset(T.land[:, 0:OWN], 0.0).then_inc(S.f3, 1)
     g.wait_ge(S.f1, 1)
-    g.affine_select(T.eye[:], T.ones[:], [[-1, 128]], AluOpType.is_equal, 0.0, 0, 1).then_inc(S.eyed, 1)
+    g.affine_select(T.sel[:], T.ones[:, 0:16], [[-32, 4], [-1, 4]], AluOpType.is_equal, 0.0, 0, 1).then_inc(S.seld, 1)
 
     def quant_w1(i):
         v.quantize_mx(T.w1q[:, 128 * i:128 * i + 128], T.w1s[:, 128 * i:128 * i + 128],
@@ -147,40 +154,43 @@ def rank_program(g, core, T, topo):
     v.wait_ge(S.la, 16)
     quant_w1(0)
     quant_w1(1)
+    v.wait_ge(S.f2, 1)
     size(0)
     v.wait_ge(S.lb, 16)
     quant_w1(2)
     quant_w1(3)
     size(1)
     size(2)
-    for i in range(3):
-        v.wait_ge(S["r%d" % i], 1)
-    v.tensor_reduce(T.m3[:], T.pm[:, 0:3], X, MAX).then_inc(S.m3d, 1)
     size(3)
-    v.wait_ge(S.f2, 1)
-    v.wait_ge(S.m3d, 1)
-    v.wait_ge(S.r3, 1)
-    v.tensor_scalar(T.bc[:], T.zero[:], T.pm[:, 3:4], T.m3[:], MAX, MAX).then_inc(S.bcd, 1)
-    pe.wait_ge(S.eyed, 1)
-    pe.wait_ge(S.bcd, 1)
-    pe.matmul(T.ps[:, 2048:2048 + 128], T.bc[:], T.eye[:], True, True).then_inc(S.tr, 1)
+    for i in range(4):
+        v.wait_ge(S["r%d" % i], 1)
+    v.transpose(T.pmt[:], T.pm[:]).then_inc(S.pmtd, 1)
+    v.wait_ge(S.pmtd, 1)
+    v.tensor_reduce(T.gm[:], T.pmt[:], X, MAX).then_inc(S.gmd, 1)
+    v.wait_ge(S.seld, 1)
+    v.wait_ge(S.gmd, 1)
+    v.tensor_scalar(T.spread[:], T.sel[:], T.gm[:], None, MULT).then_inc(S.spd, 1)
+    pe.wait_ge(S.f1, 1)
+    pe.wait_ge(S.spd, 1)
+    pe.matmul(T.ps[:, 2048:2048 + 16], T.ones[:], T.spread[:], True, True).then_inc(S.tr, 1)
     v.wait_ge(S.f3, 1)
     v.wait_ge(S.tr, 1)
-    v.tensor_reduce(T.land[:, 0:1], T.ps[:, 2048:2048 + 128], X, MAX).then_inc(S.own, 1)
+    v.tensor_reduce(T.land[:, 0:1], T.ps[:, 2048:2048 + 16], X, MAX).then_inc(S.own, 1)
 
+    mine = T.land[:, 0:1]
     g.wait_ge(S.own, 1)
-    send(g, topo, T, core, T.land[:, 0:1], [(h, T.rm[:]) for h in relays], upper, S.rmx, S.left1)
-    send(g, topo, T, core, T.land[:, 0:1], [(T.cores[d], T.land[:, slot(rank, d)]) for d in direct],
+    send(g, topo, mine, [(h, T.rm[:]) for h in relays], upper, S.mx, S.left1)
+    send(g, topo, mine, [(h, T.rm[:]) for h in remote] + [(T.cores[d], T.land[:, slot(rank, d)]) for d in direct],
          outside, S.mx, S.left1)
     v.wait_ge(S.lw, 16)
     v.quantize_mx(T.w2q[:], T.w2s[:], T.w2t[:]).then_inc(S.qw, 1)
     v.wait_ge(S.own, 1)
-    arrive = 0
-    for s in range(N):
-        if s != rank:
-            via = ways[s][rank]
-            arrive += count(topo.mask(T.cores[s] if via is None else via, core))
-    v.wait_ge(S.mx, arrive)
+
+    def engines(s):
+        via = ways[s][rank]
+        return count(topo.mask(T.cores[s] if via is None else via, core))
+
+    v.wait_ge(S.mx, sum(engines(s) for s in range(N) if s != rank))
     v.tensor_reduce(T.amax[:], T.land[:], X, MAX).then_inc(S.am, 1)
     v.wait_ge(S.am, 1)
     v.reciprocal(T.inv[:], T.amax[:]).then_inc(S.inv, 1)
@@ -198,18 +208,22 @@ def rank_program(g, core, T, topo):
     v.quantize_mx(T.hq[:, block(rank)], T.hs[:, block(rank)], T.ht[:]).then_inc(S.qh, 1)
 
     codes, scales = T.hq[:, block(rank)].bitcast(dt.uint8), T.hs[:, block(rank)]
-    g.wait_ge(S.qh, 1)
-    send(g, topo, T, core, codes, [(h, T.rq[:].bitcast(dt.uint8)) for h in relays], inside, S.rcode, S.left)
-    send(g, topo, T, core, scales, [(h, T.rs[:]) for h in relays], inside, S.rscale, S.left)
     sem = S["arr%d" % rank]
-    send(g, topo, T, core, codes, [(T.cores[d], codes) for d in direct], outside, sem, S.left)
-    send(g, topo, T, core, scales, [(T.cores[d], scales) for d in direct], outside, sem, S.left)
+    g.wait_ge(S.qh, 1)
+    total = 0
+    for there, mask in ((relays, inside), (remote, outside)):
+        if there:
+            send(g, topo, scales, [(h, T.rs[:]) for h in there], mask, S.rscale, S.left)
+            send(g, topo, codes, [(h, T.rq[:].bitcast(dt.uint8)) for h in there], mask, S.rcode, S.left)
+            total += 2 * count(mask)
+    send(g, topo, codes, [(T.cores[d], codes) for d in direct], outside, sem, S.left)
+    send(g, topo, scales, [(T.cores[d], scales) for d in direct], outside, sem, S.left)
+    total += 2 * count(outside)
     g.wait_ge(S.left1, count(upper) + count(outside))
 
-    order = ([rank] + [s for s in range(N) if s != rank and ways[s][rank] is None]
-             + [s for s in range(N) if s != rank and ways[s][rank] is not None])
+    order = [rank] + [int(s) for s in TURN[rank]]
     banks = [5, 6, 7, 0, 1, 2, 3, 4]
-    sp.wait_ge(S.left, 2 * count(inside) + 2 * count(outside))
+    sp.wait_ge(S.left, total)
     for b in range(4):
         sp.wait_ge(S["sc%d" % b], 1)
     sp.dma_start(T.h[:], T.ht[:]).then_inc(S.stored, 16)
@@ -218,8 +232,7 @@ def rank_program(g, core, T, topo):
         if s == rank:
             pe.wait_ge(S.qh, 1)
         else:
-            via = ways[s][rank]
-            pe.wait_ge(S["arr%d" % s], 2 * count(topo.mask(T.cores[s] if via is None else via, core)))
+            pe.wait_ge(S["arr%d" % s], 2 * engines(s))
         last = k == N - 1
         parts = ([(NC * s, NC // 2, k), (NC * s + NC // 2, NC // 2, k + 1)] if last else [(NC * s, NC, k)])
         for c0, n, m in parts:
@@ -237,19 +250,17 @@ def rank_program(g, core, T, topo):
     sp.wait_ge(S.stored, 16 * (N + 1))
 
 
-def relay(g, core, T, topo, s, to):
+def relay(g, core, T, topo, ways, s, to):
     S = T.sem
-    src = T.cores[s]
-    first = [d for d in range(N) if d != s and topo.same_plane(topo.chip(src), topo.chip(T.cores[d]))][0]
-    inside = topo.mask(src, core)
-    upper = inside & ~topo.mask(src, T.cores[first])
+    inside, outside, upper = masks(T, topo, ways[s], s)
+    here = topo.chip(core) == topo.chip(T.cores[s])
     mask = topo.mask(core, T.cores[to[0]])
-    g.wait_ge(S.rmx, count(upper))
-    send(g, topo, T, core, T.rm[:], [(T.cores[d], T.land[:, slot(s, d)]) for d in to], mask, S.mx, S.left)
+    g.wait_ge(S.mx, count(upper if here else outside))
+    send(g, topo, T.rm[:], [(T.cores[d], T.land[:, slot(s, d)]) for d in to], mask, S.mx, S.left)
     sem = S["arr%d" % s]
-    g.wait_ge(S.rcode, count(inside))
-    send(g, topo, T, core, T.rq[:].bitcast(dt.uint8),
+    g.wait_ge(S.rscale, count(inside if here else outside))
+    send(g, topo, T.rs[:], [(T.cores[d], T.hs[:, block(s)]) for d in to], mask, sem, S.left)
+    g.wait_ge(S.rcode, count(inside if here else outside))
+    send(g, topo, T.rq[:].bitcast(dt.uint8),
          [(T.cores[d], T.hq[:, block(s)].bitcast(dt.uint8)) for d in to], mask, sem, S.left)
-    g.wait_ge(S.rscale, count(inside))
-    send(g, topo, T, core, T.rs[:], [(T.cores[d], T.hs[:, block(s)]) for d in to], mask, sem, S.left)
     g.wait_ge(S.left, 3 * count(mask))

@@ -4,6 +4,8 @@ from concourse.mybir import dt, AluOpType, AxisListType, ActivationFunctionType
 N = 7
 NC = 256
 OWN = 4
+HUBS = {3: (2, 4, 0, 3), 4: (0, 3, 5), 2: (1, 6)}
+EARLY = ("n1 f5", "f5 g6", "n4 f4", "g6 n5", "n2 f2", "f1 n6", "g1 f5")
 WAYS = ("2n 4n 3f 5D 1D 6f",
         "3D 2f 6g 0f 5D 4g",
         "6f 0M 5f 4D 1n 3n",
@@ -26,23 +28,31 @@ SCRATCH = {
     "ones": ("sbuf", [128, 128], "float32"),
     "sel": ("sbuf", [128, 16], "float32"),
     "pm": ("sbuf", [128, 32], "float32"),
+    "pmE": ("sbuf", [128, 32], "float32"),
     "pmt": ("sbuf", [128, 32], "float32"),
+    "pmtE": ("sbuf", [128, 32], "float32"),
     "gm": ("sbuf", [128, 1], "float32"),
+    "gmE": ("sbuf", [128, 1], "float32"),
     "spread": ("sbuf", [128, 16], "float32"),
-    "land": ("sbuf", [128, OWN + N - 1], "float32"),
+    "spreadE": ("sbuf", [128, 16], "float32"),
+    "early": ("sbuf", [128, 4], "float32"),
+    "land": ("sbuf", [128, OWN + N], "float32"),
+    "part": ("sbuf", [128, 1], "float32"),
+    "hubin": ("sbuf", [128, N], "float32"),
+    "hubout": ("sbuf", [128, 1], "float32"),
     "amax": ("sbuf", [128, 1], "float32"),
     "inv": ("sbuf", [128, 1], "float32"),
     "ht": ("sbuf", [128, 4 * NC], "bfloat16"),
     "hq": ("sbuf", [128, N * NC], "float8_e4m3fn_x4"),
     "hs": ("sbuf", [128, N * NC], "uint8"),
     "yt": ("sbuf", [128, N * NC], "float32"),
-    "rm": ("sbuf", [128, 1], "float32"),
     "rq": ("sbuf", [128, NC], "float8_e4m3fn_x4"),
     "rs": ("sbuf", [128, NC], "uint8"),
     "ps": ("psum", [128, 512 * 8], "float32"),
 }
-SEMAPHORES = (["lx", "la", "lb", "lw", "f1", "f2", "f3", "seld", "qx", "qw", "qh", "pmtd", "gmd", "spd", "tr", "own",
-               "mx", "am", "inv", "stored", "left", "left1", "rcode", "rscale"]
+SEMAPHORES = (["lx", "la", "lb", "lw", "f1", "f2", "f2E", "f3", "seld", "qx", "qw", "qh", "pmtd", "gmd", "spd", "tr",
+               "pmtdE", "gmdE", "spdE", "trE", "cpE", "ownE", "ep",
+               "own", "ownq", "mx", "am", "inv", "stored", "left", "left1", "rcode", "rscale", "part", "hi", "ho"]
               + ["q%d" % i for i in range(4)] + ["z%d" % i for i in range(4)] + ["r%d" % i for i in range(4)]
               + ["sc%d" % i for i in range(4)] + ["arr%d" % i for i in range(N)]
               + ["p%d" % i for i in range(N + 1)] + ["c%d" % i for i in range(N + 1)])
@@ -53,13 +63,19 @@ def mate_port_cores(chip, topo):
     return [c for c in every if topo.chip(c) == chip and all(topo.may_write(c, d) for d in every if d != c)]
 
 
+def on_chip(T, topo, s):
+    me = T.cores[s]
+    own = mate_port_cores(topo.chip(me), topo)
+    near = [c for c in own if c != me and topo.die(c) == topo.die(me)]
+    far = [c for c in own if topo.die(c) != topo.die(me)]
+    return {"n": near[0], "f": far[0], "g": far[1]}
+
+
 def plan(T, topo):
     ways = []
     for s in range(N):
         me = T.cores[s]
-        own = mate_port_cores(topo.chip(me), topo)
-        near = [c for c in own if c != me and topo.die(c) == topo.die(me)]
-        far = [c for c in own if topo.die(c) != topo.die(me)]
+        own = on_chip(T, topo, s)
         w = {}
         for way in WAYS[s].split():
             d, how = int(way[0]), way[1]
@@ -69,9 +85,43 @@ def plan(T, topo):
                 mate = [c for c in range(topo.CHIPS) if topo.mates(c, topo.chip(T.cores[d]))][0]
                 w[d] = [c for c in mate_port_cores(mate, topo) if (topo.die(c) == topo.die(me)) == (how == "m")][0]
             else:
-                w[d] = {"n": near[0], "f": far[0], "g": far[1]}[how]
+                w[d] = own[how]
         ways.append(w)
     return ways
+
+
+def peers(T, topo, s):
+    return [d for d in range(N) if topo.same_plane(topo.chip(T.cores[s]), topo.chip(T.cores[d]))]
+
+
+def early(T, topo, s):
+    own = on_chip(T, topo, s)
+    return [(own[e[0]], int(e[1])) for e in EARLY[s].split()]
+
+
+def early_sources(T, topo, d):
+    return [(s, h) for s in range(N) for h, to in early(T, topo, s) if to == d]
+
+
+def hub_core(T, topo, r):
+    return on_chip(T, topo, r)["n"]
+
+
+def hub_ranks(T, topo, r):
+    return sorted(peers(T, topo, r) + [r])
+
+
+def hubs_of(T, topo, s):
+    hubs = [r for r in HUBS if s in hub_ranks(T, topo, r)]
+    return [r for r in hubs if r != s] + [r for r in hubs if r == s]
+
+
+def one_hop(T, topo, s):
+    return [d for d in peers(T, topo, s) if not any(d in HUBS[r] for r in hubs_of(T, topo, s))]
+
+
+def number_sources(T, topo, d):
+    return [s for s in peers(T, topo, d) if d in one_hop(T, topo, s)], [r for r in HUBS if d in HUBS[r]]
 
 
 def count(mask):
@@ -87,8 +137,7 @@ def send(g, topo, src, dsts, mask, sem, left):
                                           dsts=[ap for _, ap in dsts], alu_op=0)], local_sem=left)
 
 
-def slot(s, r):
-    k = OWN + (s if s < r else s - 1)
+def col(k):
     return slice(k, k + 1)
 
 
@@ -100,7 +149,21 @@ def masks(T, topo, w, rank):
     me = T.cores[rank]
     inside = [topo.mask(me, h) for h in w.values() if h is not None and topo.chip(h) == topo.chip(me)][0]
     outside = [topo.mask(me, T.cores[d]) for d in w if w[d] is None][0]
-    return inside, outside, inside & ~outside
+    return inside, outside
+
+
+def everywhere(g, T, c0, e=""):
+    S, v, pe = T.sem, g.vector, g.tensor
+    v.transpose(T["pmt" + e][:], T["pm" + e][:]).then_inc(S["pmtd" + e], 1)
+    v.wait_ge(S["pmtd" + e], 1)
+    v.tensor_reduce(T["gm" + e][:], T["pmt" + e][:], AxisListType.X, AluOpType.max).then_inc(S["gmd" + e], 1)
+    v.wait_ge(S.seld, 1)
+    v.wait_ge(S["gmd" + e], 1)
+    v.tensor_scalar(T["spread" + e][:], T.sel[:], T["gm" + e][:], None, AluOpType.mult).then_inc(S["spd" + e], 1)
+    pe.wait_ge(S.f1, 1)
+    pe.wait_ge(S["spd" + e], 1)
+    pe.matmul(T.ps[:, c0:c0 + 16], T.ones[:], T["spread" + e][:], True, True).then_inc(S["tr" + e], 1)
+    v.wait_ge(S["tr" + e], 1)
 
 
 def rank_program(g, core, T, topo):
@@ -122,7 +185,12 @@ def rank_program(g, core, T, topo):
     for h in w.values():
         if h is not None and h not in relays + remote:
             (relays if topo.chip(h) == topo.chip(core) else remote).append(h)
-    inside, outside, upper = masks(T, topo, w, rank)
+    inside, outside = masks(T, topo, w, rank)
+    mine = early(T, topo, rank)
+    halves = sorted(set(d for _, d in mine))
+    wholes = [d for d in one_hop(T, topo, rank) if d not in halves]
+    stages = 1 if len(halves) == len(mine) else len(mine)
+    came = early_sources(T, topo, rank)
 
     sp.dma_start(T.xt[:], T.x[:]).then_inc(S.lx, 16)
     act.dma_start(T.w1t[:, 0:1024], T.w1[:, 0:1024]).then_inc(S.la, 16)
@@ -131,9 +199,11 @@ def rank_program(g, core, T, topo):
 
     v.memset(T.ones[:], 1.0).then_inc(S.f1, 1)
     v.memset(T.pm[:], 0.0).then_inc(S.f2, 1)
+    if came:
+        v.memset(T.pmE[:], 0.0).then_inc(S.f2E, 1)
     v.memset(T.land[:, 0:OWN], 0.0).then_inc(S.f3, 1)
     g.wait_ge(S.f1, 1)
-    g.affine_select(T.sel[:], T.ones[:, 0:16], [[-32, 4], [-1, 4]], AluOpType.is_equal, 0.0, 0, 1).then_inc(S.seld, 1)
+    g.affine_select(T.sel[:], T.ones[:, 0:16], [[-1, 4], [-32, 4]], AluOpType.is_equal, 0.0, 0, 1).then_inc(S.seld, 1)
 
     def quant_w1(i):
         v.quantize_mx(T.w1q[:, 128 * i:128 * i + 128], T.w1s[:, 128 * i:128 * i + 128],
@@ -164,34 +234,46 @@ def rank_program(g, core, T, topo):
     size(3)
     for i in range(4):
         v.wait_ge(S["r%d" % i], 1)
-    v.transpose(T.pmt[:], T.pm[:]).then_inc(S.pmtd, 1)
-    v.wait_ge(S.pmtd, 1)
-    v.tensor_reduce(T.gm[:], T.pmt[:], X, MAX).then_inc(S.gmd, 1)
-    v.wait_ge(S.seld, 1)
-    v.wait_ge(S.gmd, 1)
-    v.tensor_scalar(T.spread[:], T.sel[:], T.gm[:], None, MULT).then_inc(S.spd, 1)
-    pe.wait_ge(S.f1, 1)
-    pe.wait_ge(S.spd, 1)
-    pe.matmul(T.ps[:, 2048:2048 + 16], T.ones[:], T.spread[:], True, True).then_inc(S.tr, 1)
+    everywhere(g, T, 2048)
     v.wait_ge(S.f3, 1)
-    v.wait_ge(S.tr, 1)
     v.tensor_reduce(T.land[:, 0:1], T.ps[:, 2048:2048 + 16], X, MAX).then_inc(S.own, 1)
+    v.tensor_reduce(T.land[:, 1:2], T.ps[:, 2048 + 4 * stages:2048 + 16], X, MAX).then_inc(S.ownq, 1)
 
-    mine = T.land[:, 0:1]
+    left1 = 0
+    for i in range(stages):
+        g.wait_ge(S["r%d" % i], 1)
+        send(g, topo, T.pm[:, i:i + 1], [(h, T.part[:]) for h, _ in (mine if stages == 1 else mine[i:i + 1])],
+             inside, S.part, S.left1)
+        left1 += count(inside)
     g.wait_ge(S.own, 1)
-    send(g, topo, mine, [(h, T.rm[:]) for h in relays], upper, S.mx, S.left1)
-    send(g, topo, mine, [(h, T.rm[:]) for h in remote] + [(T.cores[d], T.land[:, slot(rank, d)]) for d in direct],
-         outside, S.mx, S.left1)
+    for r in hubs_of(T, topo, rank):
+        mask = topo.mask(core, hub_core(T, topo, r))
+        send(g, topo, T.land[:, 0:1], [(hub_core(T, topo, r), T.hubin[:, col(hub_ranks(T, topo, r).index(rank))])],
+             mask, S.hi, S.left1)
+        left1 += count(mask)
+    for there, src, sem in ((wholes, T.land[:, 0:1], S.own), (halves, T.land[:, 1:2], S.ownq)):
+        g.wait_ge(sem, 1)
+        if there:
+            send(g, topo, src,
+                 [(T.cores[d], T.land[:, col(OWN + number_sources(T, topo, d)[0].index(rank))]) for d in there],
+                 outside, S.mx, S.left1)
+            left1 += count(outside)
     v.wait_ge(S.lw, 16)
     v.quantize_mx(T.w2q[:], T.w2s[:], T.w2t[:]).then_inc(S.qw, 1)
+    v.wait_ge(S.ownq, 1)
     v.wait_ge(S.own, 1)
-
-    def engines(s):
-        via = ways[s][rank]
-        return count(topo.mask(T.cores[s] if via is None else via, core))
-
-    v.wait_ge(S.mx, sum(engines(s) for s in range(N) if s != rank))
-    v.tensor_reduce(T.amax[:], T.land[:], X, MAX).then_inc(S.am, 1)
+    if came:
+        v.wait_ge(S.f2E, 1)
+        v.wait_ge(S.ep, sum(count(topo.mask(h, core)) for _, h in came))
+        v.tensor_reduce(T.pmE[:, 0:1], T["early"][:, 0:len(came)], X, MAX).then_inc(S.cpE, 1)
+        v.wait_ge(S.cpE, 1)
+        everywhere(g, T, 2048 + 16, "E")
+        v.tensor_reduce(T.land[:, 2:3], T.ps[:, 2048 + 16:2048 + 32], X, MAX).then_inc(S.ownE, 1)
+        v.wait_ge(S.ownE, 1)
+    ranks, hubs = number_sources(T, topo, rank)
+    v.wait_ge(S.mx, sum(count(topo.mask(T.cores[d], core)) for d in ranks)
+              + sum(count(topo.mask(hub_core(T, topo, r), T.cores[HUBS[r][0]])) for r in hubs))
+    v.tensor_reduce(T.amax[:], T.land[:, 0:OWN + len(ranks) + len(hubs)], X, MAX).then_inc(S.am, 1)
     v.wait_ge(S.am, 1)
     v.reciprocal(T.inv[:], T.amax[:]).then_inc(S.inv, 1)
 
@@ -219,7 +301,11 @@ def rank_program(g, core, T, topo):
     send(g, topo, codes, [(T.cores[d], codes) for d in direct], outside, sem, S.left)
     send(g, topo, scales, [(T.cores[d], scales) for d in direct], outside, sem, S.left)
     total += 2 * count(outside)
-    g.wait_ge(S.left1, count(upper) + count(outside))
+    g.wait_ge(S.left1, left1)
+
+    def engines(s):
+        via = ways[s][rank]
+        return count(topo.mask(T.cores[s] if via is None else via, core))
 
     order = [rank] + [int(s) for s in TURN[rank]]
     banks = [5, 6, 7, 0, 1, 2, 3, 4]
@@ -251,16 +337,32 @@ def rank_program(g, core, T, topo):
 
 
 def relay(g, core, T, topo, ways, s, to):
-    S = T.sem
-    inside, outside, upper = masks(T, topo, ways[s], s)
+    S, v = T.sem, g.vector
+    inside, outside = masks(T, topo, ways[s], s)
     here = topo.chip(core) == topo.chip(T.cores[s])
     mask = topo.mask(core, T.cores[to[0]])
-    g.wait_ge(S.mx, count(upper if here else outside))
-    send(g, topo, T.rm[:], [(T.cores[d], T.land[:, slot(s, d)]) for d in to], mask, S.mx, S.left)
+    calls = 2
+    for h, d in early(T, topo, s):
+        if h == core:
+            k = early_sources(T, topo, d).index((s, h))
+            g.wait_ge(S.part, count(inside))
+            send(g, topo, T.part[:], [(T.cores[d], T["early"][:, col(k)])], mask, S.ep, S.left)
+            calls += 1
+    if s in HUBS and hub_core(T, topo, s) == core:
+        ranks = hub_ranks(T, topo, s)
+        v.wait_ge(S.hi, sum(count(topo.mask(T.cores[r], core)) for r in ranks))
+        v.tensor_reduce(T.hubout[:], T.hubin[:, 0:len(ranks)], AxisListType.X, AluOpType.max).then_inc(S.ho, 1)
+        g.wait_ge(S.ho, 1)
+        dsts = []
+        for d in HUBS[s]:
+            before, hubs = number_sources(T, topo, d)
+            dsts.append((T.cores[d], T.land[:, col(OWN + len(before) + hubs.index(s))]))
+        send(g, topo, T.hubout[:], dsts, mask, S.mx, S.left)
+        calls += 1
     sem = S["arr%d" % s]
     g.wait_ge(S.rscale, count(inside if here else outside))
     send(g, topo, T.rs[:], [(T.cores[d], T.hs[:, block(s)]) for d in to], mask, sem, S.left)
     g.wait_ge(S.rcode, count(inside if here else outside))
     send(g, topo, T.rq[:].bitcast(dt.uint8),
          [(T.cores[d], T.hq[:, block(s)].bitcast(dt.uint8)) for d in to], mask, sem, S.left)
-    g.wait_ge(S.left, 3 * count(mask))
+    g.wait_ge(S.left, calls * count(mask))

from concourse.bass import DstId, RemoteDMATransfer
from concourse.mybir import dt, AluOpType, AxisListType, ActivationFunctionType

N = 7
NC = 256
OWN = 4
HUBS = {3: (2, 4, 0, 3), 4: (0, 3, 5), 2: (1, 6)}
EARLY = ("n1 f5", "f5 g6", "n4 f4", "g6 n5", "n2 f2", "f1 n6", "g1 f5")
WAYS = ("2n 4n 3f 5D 1D 6f",
        "3D 2f 6g 0f 5D 4g",
        "6f 0M 5f 4D 1n 3n",
        "1g 5D 6D 2g 0n 4n",
        "6n 0f 1f 5m 3n 2D",
        "6D 4n 1f 3f 2n 0D",
        "3g 2g 0D 1D 4f 5f")
TURN = ("654132", "350264", "104356", "160425", "652310", "031264", "524130")

SCRATCH = {
    "xt": ("sbuf", [128, 4 * NC], "bfloat16"),
    "w1t": ("sbuf", [128, 2048], "bfloat16"),
    "w2t": ("sbuf", [128, 512], "bfloat16"),
    "xq": ("sbuf", [128, NC], "float8_e4m3fn_x4"),
    "xs": ("sbuf", [128, NC], "uint8"),
    "w1q": ("sbuf", [128, 512], "float8_e4m3fn_x4"),
    "w1s": ("sbuf", [128, 512], "uint8"),
    "w2q": ("sbuf", [128, 128], "float8_e4m3fn_x4"),
    "w2s": ("sbuf", [128, 128], "uint8"),
    "ones": ("sbuf", [128, 128], "float32"),
    "sel": ("sbuf", [128, 16], "float32"),
    "pm": ("sbuf", [128, 32], "float32"),
    "pmE": ("sbuf", [128, 32], "float32"),
    "pmt": ("sbuf", [128, 32], "float32"),
    "pmtE": ("sbuf", [128, 32], "float32"),
    "gm": ("sbuf", [128, 1], "float32"),
    "gmE": ("sbuf", [128, 1], "float32"),
    "spread": ("sbuf", [128, 16], "float32"),
    "spreadE": ("sbuf", [128, 16], "float32"),
    "early": ("sbuf", [128, 4], "float32"),
    "land": ("sbuf", [128, OWN + N], "float32"),
    "part": ("sbuf", [128, 1], "float32"),
    "hubin": ("sbuf", [128, N], "float32"),
    "hubout": ("sbuf", [128, 1], "float32"),
    "amax": ("sbuf", [128, 1], "float32"),
    "inv": ("sbuf", [128, 1], "float32"),
    "ht": ("sbuf", [128, 4 * NC], "bfloat16"),
    "hq": ("sbuf", [128, N * NC], "float8_e4m3fn_x4"),
    "hs": ("sbuf", [128, N * NC], "uint8"),
    "yt": ("sbuf", [128, N * NC], "float32"),
    "rq": ("sbuf", [128, NC], "float8_e4m3fn_x4"),
    "rs": ("sbuf", [128, NC], "uint8"),
    "ps": ("psum", [128, 512 * 8], "float32"),
}
SEMAPHORES = (["lx", "la", "lb", "lw", "f1", "f2", "f2E", "f3", "seld", "qx", "qw", "qh", "pmtd", "gmd", "spd", "tr",
               "pmtdE", "gmdE", "spdE", "trE", "cpE", "ownE", "ep",
               "own", "ownq", "mx", "am", "inv", "stored", "left", "left1", "rcode", "rscale", "part", "hi", "ho"]
              + ["q%d" % i for i in range(4)] + ["z%d" % i for i in range(4)] + ["r%d" % i for i in range(4)]
              + ["sc%d" % i for i in range(4)] + ["arr%d" % i for i in range(N)]
              + ["p%d" % i for i in range(N + 1)] + ["c%d" % i for i in range(N + 1)])


def mate_port_cores(chip, topo):
    every = range(topo.CHIPS * topo.CORES_PER_CHIP)
    return [c for c in every if topo.chip(c) == chip and all(topo.may_write(c, d) for d in every if d != c)]


def on_chip(T, topo, s):
    me = T.cores[s]
    own = mate_port_cores(topo.chip(me), topo)
    near = [c for c in own if c != me and topo.die(c) == topo.die(me)]
    far = [c for c in own if topo.die(c) != topo.die(me)]
    return {"n": near[0], "f": far[0], "g": far[1]}


def plan(T, topo):
    ways = []
    for s in range(N):
        me = T.cores[s]
        own = on_chip(T, topo, s)
        w = {}
        for way in WAYS[s].split():
            d, how = int(way[0]), way[1]
            if how == "D":
                w[d] = None
            elif how in "mM":
                mate = [c for c in range(topo.CHIPS) if topo.mates(c, topo.chip(T.cores[d]))][0]
                w[d] = [c for c in mate_port_cores(mate, topo) if (topo.die(c) == topo.die(me)) == (how == "m")][0]
            else:
                w[d] = own[how]
        ways.append(w)
    return ways


def peers(T, topo, s):
    return [d for d in range(N) if topo.same_plane(topo.chip(T.cores[s]), topo.chip(T.cores[d]))]


def early(T, topo, s):
    own = on_chip(T, topo, s)
    return [(own[e[0]], int(e[1])) for e in EARLY[s].split()]


def early_sources(T, topo, d):
    return [(s, h) for s in range(N) for h, to in early(T, topo, s) if to == d]


def hub_core(T, topo, r):
    return on_chip(T, topo, r)["n"]


def hub_ranks(T, topo, r):
    return sorted(peers(T, topo, r) + [r])


def hubs_of(T, topo, s):
    hubs = [r for r in HUBS if s in hub_ranks(T, topo, r)]
    return [r for r in hubs if r != s] + [r for r in hubs if r == s]


def one_hop(T, topo, s):
    return [d for d in peers(T, topo, s) if not any(d in HUBS[r] for r in hubs_of(T, topo, s))]


def number_sources(T, topo, d):
    return [s for s in peers(T, topo, d) if d in one_hop(T, topo, s)], [r for r in HUBS if d in HUBS[r]]


def count(mask):
    return bin(mask).count("1")


def send(g, topo, src, dsts, mask, sem, left):
    ids = []
    for c, _ in dsts:
        rid, pid, _e = topo.addr(c)
        ids.append(DstId(rid=rid, pnc=pid))
    g.remote_dma_fused([RemoteDMATransfer(dst_ids=ids, dma_engine_mask=mask, remote_sem=sem, srcs=[src],
                                          dsts=[ap for _, ap in dsts], alu_op=0)], local_sem=left)


def col(k):
    return slice(k, k + 1)


def block(s):
    return slice(NC * s, NC * (s + 1))


def masks(T, topo, w, rank):
    me = T.cores[rank]
    inside = [topo.mask(me, h) for h in w.values() if h is not None and topo.chip(h) == topo.chip(me)][0]
    outside = [topo.mask(me, T.cores[d]) for d in w if w[d] is None][0]
    return inside, outside


def everywhere(g, T, c0, e=""):
    S, v, pe = T.sem, g.vector, g.tensor
    v.transpose(T["pmt" + e][:], T["pm" + e][:]).then_inc(S["pmtd" + e], 1)
    v.wait_ge(S["pmtd" + e], 1)
    v.tensor_reduce(T["gm" + e][:], T["pmt" + e][:], AxisListType.X, AluOpType.max).then_inc(S["gmd" + e], 1)
    v.wait_ge(S.seld, 1)
    v.wait_ge(S["gmd" + e], 1)
    v.tensor_scalar(T["spread" + e][:], T.sel[:], T["gm" + e][:], None, AluOpType.mult).then_inc(S["spd" + e], 1)
    pe.wait_ge(S.f1, 1)
    pe.wait_ge(S["spd" + e], 1)
    pe.matmul(T.ps[:, c0:c0 + 16], T.ones[:], T["spread" + e][:], True, True).then_inc(S["tr" + e], 1)
    v.wait_ge(S["tr" + e], 1)


def rank_program(g, core, T, topo):
    ways = plan(T, topo)
    rank = T.rank_of(core)
    if rank is None:
        for s in range(N):
            to = [d for d in ways[s] if ways[s][d] == core]
            if to:
                relay(g, core, T, topo, ways, s, to)
        return
    S = T.sem
    MULT, MAX = AluOpType.mult, AluOpType.max
    X, COPY = AxisListType.X, ActivationFunctionType.Copy
    v, pe, act, sp = g.vector, g.tensor, g.scalar, g.sync
    w = ways[rank]
    direct = [d for d in w if w[d] is None]
    relays, remote = [], []
    for h in w.values():
        if h is not None and h not in relays + remote:
            (relays if topo.chip(h) == topo.chip(core) else remote).append(h)
    inside, outside = masks(T, topo, w, rank)
    mine = early(T, topo, rank)
    halves = sorted(set(d for _, d in mine))
    wholes = [d for d in one_hop(T, topo, rank) if d not in halves]
    stages = 1 if len(halves) == len(mine) else len(mine)
    came = early_sources(T, topo, rank)

    sp.dma_start(T.xt[:], T.x[:]).then_inc(S.lx, 16)
    act.dma_start(T.w1t[:, 0:1024], T.w1[:, 0:1024]).then_inc(S.la, 16)
    sp.dma_start(T.w1t[:, 1024:2048], T.w1[:, 1024:2048]).then_inc(S.lb, 16)
    sp.dma_start(T.w2t[:], T.w2[:]).then_inc(S.lw, 16)

    v.memset(T.ones[:], 1.0).then_inc(S.f1, 1)
    v.memset(T.pm[:], 0.0).then_inc(S.f2, 1)
    if came:
        v.memset(T.pmE[:], 0.0).then_inc(S.f2E, 1)
    v.memset(T.land[:, 0:OWN], 0.0).then_inc(S.f3, 1)
    g.wait_ge(S.f1, 1)
    g.affine_select(T.sel[:], T.ones[:, 0:16], [[-1, 4], [-32, 4]], AluOpType.is_equal, 0.0, 0, 1).then_inc(S.seld, 1)

    def quant_w1(i):
        v.quantize_mx(T.w1q[:, 128 * i:128 * i + 128], T.w1s[:, 128 * i:128 * i + 128],
                      T.w1t[:, 512 * i:512 * i + 512]).then_inc(S["q%d" % i], 1)

    def size(i):
        v.wait_ge(S["z%d" % i], 1)
        v.tensor_reduce(T.pm[:, i:i + 1], T.ps[:, 512 * i:512 * i + NC], X, MAX,
                        apply_absolute_value=True).then_inc(S["r%d" % i], 1)

    pe.wait_ge(S.qx, 1)
    for i in range(4):
        pe.wait_ge(S["q%d" % i], 1)
        pe.matmul_mx(T.ps[:, 512 * i:512 * i + NC], T.w1q[:, 128 * i:128 * i + 128], T.w1s[:, 128 * i:128 * i + 128],
                     T.xq[:], T.xs[:], True, True).then_inc(S["z%d" % i], 1)
    v.wait_ge(S.lx, 16)
    v.quantize_mx(T.xq[:], T.xs[:], T.xt[:]).then_inc(S.qx, 1)
    v.wait_ge(S.la, 16)
    quant_w1(0)
    quant_w1(1)
    v.wait_ge(S.f2, 1)
    size(0)
    v.wait_ge(S.lb, 16)
    quant_w1(2)
    quant_w1(3)
    size(1)
    size(2)
    size(3)
    for i in range(4):
        v.wait_ge(S["r%d" % i], 1)
    everywhere(g, T, 2048)
    v.wait_ge(S.f3, 1)
    v.tensor_reduce(T.land[:, 0:1], T.ps[:, 2048:2048 + 16], X, MAX).then_inc(S.own, 1)
    v.tensor_reduce(T.land[:, 1:2], T.ps[:, 2048 + 4 * stages:2048 + 16], X, MAX).then_inc(S.ownq, 1)

    left1 = 0
    for i in range(stages):
        g.wait_ge(S["r%d" % i], 1)
        send(g, topo, T.pm[:, i:i + 1], [(h, T.part[:]) for h, _ in (mine if stages == 1 else mine[i:i + 1])],
             inside, S.part, S.left1)
        left1 += count(inside)
    g.wait_ge(S.own, 1)
    for r in hubs_of(T, topo, rank):
        mask = topo.mask(core, hub_core(T, topo, r))
        send(g, topo, T.land[:, 0:1], [(hub_core(T, topo, r), T.hubin[:, col(hub_ranks(T, topo, r).index(rank))])],
             mask, S.hi, S.left1)
        left1 += count(mask)
    for there, src, sem in ((wholes, T.land[:, 0:1], S.own), (halves, T.land[:, 1:2], S.ownq)):
        g.wait_ge(sem, 1)
        if there:
            send(g, topo, src,
                 [(T.cores[d], T.land[:, col(OWN + number_sources(T, topo, d)[0].index(rank))]) for d in there],
                 outside, S.mx, S.left1)
            left1 += count(outside)
    v.wait_ge(S.lw, 16)
    v.quantize_mx(T.w2q[:], T.w2s[:], T.w2t[:]).then_inc(S.qw, 1)
    v.wait_ge(S.ownq, 1)
    v.wait_ge(S.own, 1)
    if came:
        v.wait_ge(S.f2E, 1)
        v.wait_ge(S.ep, sum(count(topo.mask(h, core)) for _, h in came))
        v.tensor_reduce(T.pmE[:, 0:1], T["early"][:, 0:len(came)], X, MAX).then_inc(S.cpE, 1)
        v.wait_ge(S.cpE, 1)
        everywhere(g, T, 2048 + 16, "E")
        v.tensor_reduce(T.land[:, 2:3], T.ps[:, 2048 + 16:2048 + 32], X, MAX).then_inc(S.ownE, 1)
        v.wait_ge(S.ownE, 1)
    ranks, hubs = number_sources(T, topo, rank)
    v.wait_ge(S.mx, sum(count(topo.mask(T.cores[d], core)) for d in ranks)
              + sum(count(topo.mask(hub_core(T, topo, r), T.cores[HUBS[r][0]])) for r in hubs))
    v.tensor_reduce(T.amax[:], T.land[:, 0:OWN + len(ranks) + len(hubs)], X, MAX).then_inc(S.am, 1)
    v.wait_ge(S.am, 1)
    v.reciprocal(T.inv[:], T.amax[:]).then_inc(S.inv, 1)

    v.wait_ge(S.inv, 1)
    act.wait_ge(S.inv, 1)
    for b in (0, 1):
        v.tensor_scalar(T.ht[:, b:4 * NC:4], T.ps[:, 512 * b:512 * b + NC], T.inv[:], None,
                        MULT).then_inc(S["sc%d" % b], 1)
    for b in (2, 3):
        act.activation(T.ht[:, b:4 * NC:4], T.ps[:, 512 * b:512 * b + NC], COPY,
                       scale=T.inv[:]).then_inc(S["sc%d" % b], 1)
    for b in range(4):
        v.wait_ge(S["sc%d" % b], 1)
    v.quantize_mx(T.hq[:, block(rank)], T.hs[:, block(rank)], T.ht[:]).then_inc(S.qh, 1)

    codes, scales = T.hq[:, block(rank)].bitcast(dt.uint8), T.hs[:, block(rank)]
    sem = S["arr%d" % rank]
    g.wait_ge(S.qh, 1)
    total = 0
    for there, mask in ((relays, inside), (remote, outside)):
        if there:
            send(g, topo, scales, [(h, T.rs[:]) for h in there], mask, S.rscale, S.left)
            send(g, topo, codes, [(h, T.rq[:].bitcast(dt.uint8)) for h in there], mask, S.rcode, S.left)
            total += 2 * count(mask)
    send(g, topo, codes, [(T.cores[d], codes) for d in direct], outside, sem, S.left)
    send(g, topo, scales, [(T.cores[d], scales) for d in direct], outside, sem, S.left)
    total += 2 * count(outside)
    g.wait_ge(S.left1, left1)

    def engines(s):
        via = ways[s][rank]
        return count(topo.mask(T.cores[s] if via is None else via, core))

    order = [rank] + [int(s) for s in TURN[rank]]
    banks = [5, 6, 7, 0, 1, 2, 3, 4]
    sp.wait_ge(S.left, total)
    for b in range(4):
        sp.wait_ge(S["sc%d" % b], 1)
    sp.dma_start(T.h[:], T.ht[:]).then_inc(S.stored, 16)
    pe.wait_ge(S.qw, 1)
    for k, s in enumerate(order):
        if s == rank:
            pe.wait_ge(S.qh, 1)
        else:
            pe.wait_ge(S["arr%d" % s], 2 * engines(s))
        last = k == N - 1
        parts = ([(NC * s, NC // 2, k), (NC * s + NC // 2, NC // 2, k + 1)] if last else [(NC * s, NC, k)])
        for c0, n, m in parts:
            out = T.ps[:, 512 * banks[m]:512 * banks[m] + n]
            pe.matmul_mx(out, T.w2q[:], T.w2s[:], T.hq[:, c0:c0 + n], T.hs[:, c0:c0 + n],
                         True, True).then_inc(S["p%d" % m], 1)
            if m % 2 == 0:
                v.wait_ge(S["p%d" % m], 1)
                v.tensor_copy(T.yt[:, c0:c0 + n], out).then_inc(S["c%d" % m], 1)
            else:
                act.wait_ge(S["p%d" % m], 1)
                act.activation(T.yt[:, c0:c0 + n], out, COPY).then_inc(S["c%d" % m], 1)
            sp.wait_ge(S["c%d" % m], 1)
        sp.dma_start(T.y[:, block(s)], T.yt[:, block(s)]).then_inc(S.stored, 16)
    sp.wait_ge(S.stored, 16 * (N + 1))


def relay(g, core, T, topo, ways, s, to):
    S, v = T.sem, g.vector
    inside, outside = masks(T, topo, ways[s], s)
    here = topo.chip(core) == topo.chip(T.cores[s])
    mask = topo.mask(core, T.cores[to[0]])
    calls = 2
    for h, d in early(T, topo, s):
        if h == core:
            k = early_sources(T, topo, d).index((s, h))
            g.wait_ge(S.part, count(inside))
            send(g, topo, T.part[:], [(T.cores[d], T["early"][:, col(k)])], mask, S.ep, S.left)
            calls += 1
    if s in HUBS and hub_core(T, topo, s) == core:
        ranks = hub_ranks(T, topo, s)
        v.wait_ge(S.hi, sum(count(topo.mask(T.cores[r], core)) for r in ranks))
        v.tensor_reduce(T.hubout[:], T.hubin[:, 0:len(ranks)], AxisListType.X, AluOpType.max).then_inc(S.ho, 1)
        g.wait_ge(S.ho, 1)
        dsts = []
        for d in HUBS[s]:
            before, hubs = number_sources(T, topo, d)
            dsts.append((T.cores[d], T.land[:, col(OWN + len(before) + hubs.index(s))]))
        send(g, topo, T.hubout[:], dsts, mask, S.mx, S.left)
        calls += 1
    sem = S["arr%d" % s]
    g.wait_ge(S.rscale, count(inside if here else outside))
    send(g, topo, T.rs[:], [(T.cores[d], T.hs[:, block(s)]) for d in to], mask, sem, S.left)
    g.wait_ge(S.rcode, count(inside if here else outside))
    send(g, topo, T.rq[:].bitcast(dt.uint8),
         [(T.cores[d], T.hq[:, block(s)].bitcast(dt.uint8)) for d in to], mask, sem, S.left)
    g.wait_ge(S.left, calls * count(mask))
